import numpy as np
CORES = [6,22,38,54,70,86,102,118]
N = 8
T = 4
ROUTE = [[[0,4],[0,4],[1,5],[4,6]],[[3,0],[0,3],[3,6],[3,0]],[[7,1],[0,7],[0,4],[7,0]],[[0,2],[0,7],[7,0],[0,7]],[[0,5],[0,7],[6,0],[0,4]],[[0,4],[0,4],[0,1],[0,2]],[[7,0],[6,0],[0,5],[0,4]],[[5,0],[0,7],[0,7],[1,0]]]
CAP = 5
YW = 5
def setup_inputs(rng):
    return {"x": rng.standard_normal((N, 128, T), dtype=np.float32)}
def reference(x):
    y = np.full((N, 128, YW), np.nan, x.dtype)
    fill = [0] * N
    for r in range(N):
        for t in range(T):
            for e in ROUTE[r][t]:
                if fill[e] < CAP:
                    y[e][:, fill[e]] = x[r][:, t]
                fill[e] += 1
    return {"y": y}

from concourse.bass import DstId, RemoteDMATransfer

SCRATCH = {
    "xs": ("sbuf", [128, 4], "float32"),
    "land": ("sbuf", [128, 5], "float32"),
}
SEMAPHORES = ["loaded", "kept", "left", "arrived", "stored"]


def make_plan(tables, n):
    route, cap = tables["ROUTE"], tables["CAP"]
    fill = [0] * n
    runs = [[] for _ in range(n)]
    for r in range(n):
        last = {}
        for t in range(len(route[r])):
            for e in route[r][t]:
                s = fill[e]
                fill[e] += 1
                if s >= cap:
                    continue
                if e in last:
                    e0, t0, s0, w = runs[r][last[e]]
                    if t0 + w == t:
                        runs[r][last[e]] = (e, t0, s0, w + 1)
                        continue
                last[e] = len(runs[r])
                runs[r].append((e, t, s, 1))
    return runs, [min(f, cap) for f in fill]


def make_calls(runs_r, r):
    calls = []
    for w in sorted({q[3] for q in runs_r if q[0] != r}):
        grp = [q for q in runs_r if q[0] != r and q[3] == w]
        for i in range(0, len(grp), 8):
            part = grp[i:i + 8]
            ne = 8
            while ne * len(part) > 8:
                ne //= 2
            calls.append([(e, t0, s0, w, ((1 << ne) - 1) << (k * ne), ne)
                          for k, (e, t0, s0, w) in enumerate(part)])
    return calls


def rank_program(g, core, T, topo):
    rank = T.rank_of(core)
    if rank is None:
        return
    n = len(T.cores)
    runs, count = make_plan(T.tables, n)
    calls = [make_calls(runs[r], r) for r in range(n)]

    if calls[rank]:
        g.sync.dma_start(T.xs[:], T.x[:]).then_inc(T.sem.loaded, 16)
    kept = 0
    for e, t0, s0, w in runs[rank]:
        if e == rank:
            g.dma_start(T.land[:, s0:s0 + w], T.x[:, t0:t0 + w],
                        allow_slow_non_contiguous=(w == 1)).then_inc(T.sem.kept, 16)
            kept += 16

    left = 0
    if calls[rank]:
        g.wait_ge(T.sem.loaded, 16)
    for call in calls[rank]:
        trs = []
        for e, t0, s0, w, mask, ne in call:
            rid, pid, _se = topo.addr(T.cores[e])
            trs.append(RemoteDMATransfer(dst_ids=[DstId(rid=rid, pnc=pid)], dma_engine_mask=mask,
                                         remote_sem=T.sem.arrived,
                                         src=T.xs[:, t0:t0 + w], dst=T.land[:, s0:s0 + w]))
            left += ne
        g.remote_dma_fused(trs, local_sem=T.sem.left)

    arrive = sum(q[5] for r in range(n) for call in calls[r] for q in call if q[0] == rank)
    if kept:
        g.wait_ge(T.sem.kept, kept)
    if arrive:
        g.wait_ge(T.sem.arrived, arrive)
    c = count[rank]
    if c:
        g.dma_start(T.y[:, 0:c], T.land[:, 0:c], allow_slow_non_contiguous=(c == 1)).then_inc(T.sem.stored, 16)
        g.wait_ge(T.sem.stored, 16)
    if left:
        g.wait_ge(T.sem.left, left)
